import numpy as np
import ml_dtypes


def mxq(x, axis, fmt="e4m3"):
    dtype, down = {"e4m3": (ml_dtypes.float8_e4m3fn, 7), "e5m2": (ml_dtypes.float8_e5m2, 14)}[fmt]
    v = np.moveaxis(np.asarray(x, np.float32).astype(ml_dtypes.bfloat16).astype(np.float64), axis, -1)
    blocks = v.reshape(v.shape[:-1] + (-1, 32))
    amax = np.abs(blocks).max(-1, keepdims=True)
    byte = np.maximum(np.where(amax > 0, np.frexp(amax)[1] - 1 + 127, 0) - down, 1)
    scale = np.exp2(byte - 127.0)
    codes = (blocks / scale).astype(np.float32).astype(dtype).astype(np.float64)
    return np.moveaxis((codes * scale).reshape(v.shape), -1, axis)


WIDE = False


def mx_kscale(k):
    if not WIDE:
        return np.ones(k)
    levels = np.array([10, -10, 5, -5, 0])
    if k % 512:
        return np.exp2(np.random.permutation(np.resize(levels, k // 32))).repeat(32)
    a = np.empty((k // 512, 16))
    for p in range(k // 512):
        a[p, :8] = np.random.permutation(np.resize(levels, 8))
        for g in range(8):
            far = levels[np.abs(levels - a[p, g]) >= 10]
            a[p, g + 8] = far[np.random.randint(len(far))]
    return np.exp2(a.ravel()).repeat(32)


def f64(x):
    return np.asarray(x).astype(np.float64)


def striped(idx):
    return np.tile(idx.reshape(-1, 16).T, (8, 1)).astype(np.uint16)


def unstriped(offs):
    return offs[:16].T.reshape(-1).astype(np.int64)


K, T, D, V, H, N = 2048, 512, 6, 256, 512, 128
P = 2 ** 7


def setup_inputs():
    n = np.random.standard_normal
    s = mx_kscale(K)[:, None]
    u = mx_kscale(H)
    return {
        "xT": (n((K, T)) * s).astype(np.float32),
        "w1": (n((K, H)) / np.sqrt(K) / s * u).astype(np.float32),
        "w2": (n((H, N)) / np.sqrt(H) / u[:, None]).astype(np.float32),
        "gate": np.tile(np.random.uniform(0.2, 1.0, (D, 1, V)) / np.sqrt(D), (1, P, 1)).astype(np.float32),
        "pos1": striped(np.random.permutation(T)[:V]),
        "pos2": striped(np.random.permutation(T)[:V]),
        "pos3": striped(np.random.permutation(T)[:V]),
        "pos4": striped(np.random.permutation(T)[:V]),
        "pos5": striped(np.random.permutation(T)[:V]),
        "pos6": striped(np.random.permutation(T)[:V]),
    }


def reference(xT, w1, w2, gate, pos1, pos2, pos3, pos4, pos5, pos6):
    h = mxq(f64(w1), 0, "e4m3").T @ mxq(f64(xT), 0, "e4m3")
    z = sum(f64(gate)[d, :1] * h[:, unstriped(p)] for d, p in enumerate((pos1, pos2, pos3, pos4, pos5, pos6)))
    return mxq(f64(w2), 0, "e4m3").T @ mxq(z, 0, "e4m3")

@@ -1,0 +1,200 @@
+from contextlib import ExitStack
+
+import concourse.mybir as mybir
+from concourse.masks import make_identity
+
+K, T, D, V, H, N = 2048, 512, 6, 256, 512, 128
+P = 128
+PASSES = K // 512
+BLOCKS = H // P
+HALVES = V // P
+FLOPS = 2 * K * H * T + 2 * H * N * V
+
+F32 = mybir.dt.float32
+BF16 = mybir.dt.bfloat16
+U32 = mybir.dt.uint32
+U16 = mybir.dt.uint16
+U8 = mybir.dt.uint8
+FP8X4 = mybir.dt.float8_e4m3fn_x4
+MULT = mybir.AluOpType.mult
+
+
+def tile_picked_gcn_mlp_none_sub_l_kernel(tc, xT, w1, w2, gate, pos1, pos2, pos3, pos4, pos5, pos6, out):
+    nc = tc.nc
+    lists_in = (pos1, pos2, pos3, pos4, pos5, pos6)
+
+    with ExitStack() as ctx:
+        lists = ctx.enter_context(tc.tile_pool(name="lists", bufs=1))
+        keep = ctx.enter_context(tc.tile_pool(name="keep", bufs=1))
+        ring = ctx.enter_context(tc.tile_pool(name="ring", bufs=4))
+        psum = ctx.enter_context(tc.psum_pool(name="psum", bufs=2))
+        psum1 = ctx.enter_context(tc.psum_pool(name="psum1", bufs=1))
+
+        pos = [lists.tile([P, V // 16], U16, name=f"pos{d}") for d in range(D)]
+        ident_f32 = keep.tile([P, P], F32, name="ident_f32")
+        ident_bf16 = keep.tile([P, P], BF16, name="ident_bf16")
+        make_identity(nc, ident_f32[:])
+        make_identity(nc, ident_bf16[:])
+
+        xraw = [keep.tile([P, 4, T], F32, name=f"xraw{c}") for c in range(PASSES)]
+        wraw = [[keep.tile([P, 2, 4, P], F32, name=f"wraw{b}_{s}") for s in range(2)] for b in range(BLOCKS)]
+        w2raw = keep.tile([P, 4, N], F32, name="w2raw")
+        gates = [keep.tile([P, 2, V], F32, name=f"gates{g}") for g in range(D // 2)]
+
+        def load_w1(b, c):
+            nc.sync.dma_start(
+                out=wraw[b][c // 2][:, c % 2, :, :],
+                in_=w1[512 * c : 512 * (c + 1), P * b : P * (b + 1)].rearrange("(p j) w -> p j w", j=4),
+            )
+
+        def load_list(d):
+            nc.sync.dma_start(pos[d][:], lists_in[d])
+
+        def load_gates(g):
+            nc.sync.dma_start(out=gates[g][:], in_=gate[2 * g : 2 * g + 2].rearrange("d p v -> p d v"))
+
+        for c in range(PASSES):
+            nc.sync.dma_start(out=xraw[c][:], in_=xT[512 * c : 512 * (c + 1), :].rearrange("(p j) w -> p j w", j=4))
+        for c in range(PASSES):
+            load_w1(0, c)
+        load_list(0)
+        load_gates(0)
+        load_list(1)
+        load_w1(1, 0)
+        load_list(2)
+        load_gates(1)
+        load_list(3)
+        load_w1(1, 1)
+        load_list(4)
+        load_gates(2)
+        load_list(5)
+        load_w1(1, 2)
+        load_w1(1, 3)
+        for c in range(PASSES):
+            load_w1(2, c)
+        for c in range(PASSES):
+            load_w1(3, c)
+        nc.sync.dma_start(out=w2raw[:], in_=w2.rearrange("(p j) m -> p j m", j=4))
+
+        xq = []
+        for c in range(PASSES):
+            grouped = keep.tile([P, T, 4], BF16, name=f"xg{c}", align_bytes=64)
+            codes = keep.tile([P, T], U32, name=f"xq{c}", align_bytes=64)
+            scales = keep.tile([P, T], U8, name=f"xs{c}", align_bytes=64)
+            cut = 256
+            nc.scalar.copy(
+                grouped[:, :cut, :].rearrange("p (c i) t -> p c t i", i=4),
+                xraw[c][:, :, :cut].rearrange("p t (c i) -> p c t i", i=4),
+            )
+            nc.vector.tensor_copy(
+                grouped[:, cut:, :].rearrange("p (c i) t -> p c t i", i=4),
+                xraw[c][:, :, cut:].rearrange("p t (c i) -> p c t i", i=4),
+            )
+            nc.vector.quantize_mx(out=codes[:].bitcast(FP8X4), scales=scales[:], in_=grouped[:].rearrange("p w t -> p (w t)"))
+            xq.append((codes, scales))
+
+        wg = [[keep.tile([P, 2, P, 4], BF16, name=f"wg{b}_{s}", align_bytes=64) for s in range(2)] for b in range(BLOCKS)]
+        wq = [[keep.tile([P, 2, P], U32, name=f"wq{b}_{s}", align_bytes=64) for s in range(2)] for b in range(BLOCKS)]
+        ws = [[keep.tile([P, 2, P], U8, name=f"ws{b}_{s}", align_bytes=64) for s in range(2)] for b in range(BLOCKS)]
+        h = [keep.tile([P, T], F32, name=f"h{b}") for b in range(BLOCKS)]
+        hps = {}
+
+        def multiply(b, c):
+            if c == 0:
+                hps[b] = psum.tile([P, T], F32, name="bank")
+            nc.tensor.matmul_mx(
+                out=hps[b][:],
+                lhsT=wq[b][c // 2][:, c % 2, :].bitcast(FP8X4),
+                lhsT_scale=ws[b][c // 2][:, c % 2, :],
+                rhs=xq[c][0][:].bitcast(FP8X4),
+                rhs_scale=xq[c][1][:],
+                start=(c == 0),
+                stop=(c == PASSES - 1),
+            )
+
+        for c in range(PASSES):
+            src = wraw[0][c // 2][:, c % 2, :, :]
+            dst = wg[0][c // 2][:, c % 2, :, :]
+            nc.scalar.copy(dst[:, :64, :].rearrange("p (c i) t -> p c t i", i=4), src[:, :, :64].rearrange("p t (c i) -> p c t i", i=4))
+            nc.vector.tensor_copy(dst[:, 64:, :].rearrange("p (c i) t -> p c t i", i=4), src[:, :, 64:].rearrange("p t (c i) -> p c t i", i=4))
+            nc.vector.quantize_mx(
+                out=wq[0][c // 2][:, c % 2, :].bitcast(FP8X4),
+                scales=ws[0][c // 2][:, c % 2, :],
+                in_=dst.rearrange("p w t -> p (w t)"),
+            )
+            multiply(0, c)
+        nc.scalar.copy(h[0][:], hps[0][:])
+
+        def copy_w1(b, s):
+            nc.scalar.copy(wg[b][s][:], wraw[b][s][:].rearrange("p c t w -> p c w t"))
+
+        def quantise_w1(b, s):
+            nc.vector.quantize_mx(
+                out=wq[b][s][:].rearrange("p c w -> p (c w)").bitcast(FP8X4),
+                scales=ws[b][s][:].rearrange("p c w -> p (c w)"),
+                in_=wg[b][s][:].rearrange("p c w t -> p (c w t)"),
+            )
+            multiply(b, 2 * s)
+            multiply(b, 2 * s + 1)
+
+        w2g = keep.tile([P, N, 4], BF16, name="w2g", align_bytes=64)
+        w2q = keep.tile([P, N], U32, name="w2q", align_bytes=64)
+        w2s = keep.tile([P, N], U8, name="w2s", align_bytes=64)
+        zT = [keep.tile([P, 4, P], BF16, name=f"zT{v}") for v in range(HALVES)]
+
+        for b in range(BLOCKS):
+            if b + 1 < BLOCKS:
+                copy_w1(b + 1, 0)
+                copy_w1(b + 1, 1)
+            else:
+                nc.scalar.copy(w2g[:], w2raw[:].rearrange("p t m -> p m t"))
+            acc = [psum.tile([P, P], F32, name=f"acc{v}") for v in range(HALVES)]
+            for d in range(D):
+                picked = ring.tile([P, V], F32, name="picked")
+                nc.vector.tensor_tensor(picked[:], h[b][:].indirect(pos[d][:]), gates[d // 2][:, d % 2, :], MULT)
+                for v in range(HALVES):
+                    nc.tensor.matmul(
+                        acc[v][:], picked[:, P * v : P * (v + 1)], ident_f32[:],
+                        is_transpose=True, start=(d == 0), stop=(d == D - 1),
+                    )
+                if b + 1 < BLOCKS:
+                    if d == 1:
+                        quantise_w1(b + 1, 0)
+                    if d == 4:
+                        quantise_w1(b + 1, 1)
+                        nc.scalar.copy(h[b + 1][:], hps[b + 1][:])
+                elif d == 2:
+                    nc.vector.quantize_mx(out=w2q[:].bitcast(FP8X4), scales=w2s[:], in_=w2g[:].rearrange("p m t -> p (m t)"))
+            for v in range(HALVES):
+                dst = zT[v][:, :, 32 * b : 32 * (b + 1)]
+                src = acc[v][:].rearrange("p (q t) -> p t q", t=4)
+                if v == 1 and b == BLOCKS - 1:
+                    nc.vector.tensor_copy(dst, src)
+                else:
+                    nc.scalar.copy(dst, src)
+
+        zbank = [psum1.tile([P, 4, P], BF16, name=f"zbank{v}") for v in range(HALVES)]
+        zg = [keep.tile([P, P, 4], BF16, name=f"zg{v}", align_bytes=64) for v in range(HALVES)]
+        zq = [keep.tile([P, P], U32, name=f"zq{v}", align_bytes=64) for v in range(HALVES)]
+        zs = [keep.tile([P, P], U8, name=f"zs{v}", align_bytes=64) for v in range(HALVES)]
+        result = [keep.tile([P, P], F32, name=f"result{v}") for v in range(HALVES)]
+        for v in range(HALVES):
+            for t in range(4):
+                nc.tensor.transpose(zbank[v][:, t, :], zT[v][:, t, :], ident_bf16[:])
+        nc.scalar.copy(zg[0][:], zbank[0][:].rearrange("p t v -> p v t"))
+        nc.vector.tensor_copy(zg[1][:], zbank[1][:].rearrange("p t v -> p v t"))
+        for v in range(HALVES):
+            nc.vector.quantize_mx(out=zq[v][:].bitcast(FP8X4), scales=zs[v][:], in_=zg[v][:].rearrange("p v t -> p (v t)"))
+            bank = psum.tile([P, T], F32, name="bank")
+            nc.tensor.matmul_mx(
+                out=bank[:, :P],
+                lhsT=w2q[:].bitcast(FP8X4), lhsT_scale=w2s[:],
+                rhs=zq[v][:].bitcast(FP8X4), rhs_scale=zs[v][:],
+                start=True, stop=True,
+            )
+            if v == 0:
+                nc.scalar.copy(result[v][:], bank[:, :P])
+                nc.scalar.dma_start(out=out[:, :P], in_=result[v][:])
+            else:
+                nc.vector.tensor_copy(result[v][:], bank[:, :P])
+                nc.sync.dma_start(out=out[:, P:], in_=result[v][:])

@@ -9,6 +9,7 @@ PASSES = K // 512
 BLOCKS = H // P
 HALVES = V // P
 FLOPS = 2 * K * H * T + 2 * H * N * V
+BYTES = 4 * (K * T + K * H + H * N + D * V + N * V) + 2 * D * P * (V // 16)
 
 F32 = mybir.dt.float32
 BF16 = mybir.dt.bfloat16
@@ -31,15 +32,12 @@ def tile_picked_gcn_mlp_none_sub_l_kernel(tc, xT, w1, w2, gate, pos1, pos2, pos3
         psum1 = ctx.enter_context(tc.psum_pool(name="psum1", bufs=1))
 
         pos = [lists.tile([P, V // 16], U16, name=f"pos{d}") for d in range(D)]
-        ident_f32 = keep.tile([P, P], F32, name="ident_f32")
-        ident_bf16 = keep.tile([P, P], BF16, name="ident_bf16")
-        make_identity(nc, ident_f32[:])
-        make_identity(nc, ident_bf16[:])
 
         xraw = [keep.tile([P, 4, T], F32, name=f"xraw{c}") for c in range(PASSES)]
         wraw = [[keep.tile([P, 2, 4, P], F32, name=f"wraw{b}_{s}") for s in range(2)] for b in range(BLOCKS)]
         w2raw = keep.tile([P, 4, N], F32, name="w2raw")
-        gates = [keep.tile([P, 2, V], F32, name=f"gates{g}") for g in range(D // 2)]
+        gate_rows = keep.tile([P, P], F32, name="gate_rows")
+        nc.gpsimd.memset(gate_rows[:], 0.0)
 
         def load_w1(b, c):
             nc.sync.dma_start(
@@ -50,38 +48,59 @@ def tile_picked_gcn_mlp_none_sub_l_kernel(tc, xT, w1, w2, gate, pos1, pos2, pos3
         def load_list(d):
             nc.sync.dma_start(pos[d][:], lists_in[d])
 
-        def load_gates(g):
-            nc.sync.dma_start(out=gates[g][:], in_=gate[2 * g : 2 * g + 2].rearrange("d p v -> p d v"))
-
         for c in range(PASSES):
             nc.sync.dma_start(out=xraw[c][:], in_=xT[512 * c : 512 * (c + 1), :].rearrange("(p j) w -> p j w", j=4))
+            if c == 0:
+                for v in range(HALVES):
+                    nc.sync.dma_start(out=gate_rows[D * v : D * (v + 1), :], in_=gate[:, 0, P * v : P * (v + 1)])
         for c in range(PASSES):
             load_w1(0, c)
         load_list(0)
-        load_gates(0)
         load_list(1)
         load_w1(1, 0)
         load_list(2)
-        load_gates(1)
-        load_list(3)
         load_w1(1, 1)
-        load_list(4)
-        load_gates(2)
-        load_list(5)
+        load_list(3)
         load_w1(1, 2)
+        load_list(4)
+        load_list(5)
         load_w1(1, 3)
         for c in range(PASSES):
             load_w1(2, c)
+        nc.sync.dma_start(out=w2raw[:], in_=w2.rearrange("(p j) m -> p j m", j=4))
         for c in range(PASSES):
             load_w1(3, c)
-        nc.sync.dma_start(out=w2raw[:], in_=w2.rearrange("(p j) m -> p j m", j=4))
+
+        ident = keep.tile([P, P], F32, name="ident")
+        make_identity(nc, ident[:])
+
+        def spread_gates():
+            gate_bank = psum.tile([P, T], F32, name="bank")
+            nc.tensor.transpose(gate_bank[:, :P], gate_rows[:], ident[:])
+            gate_cols = keep.tile([P, D * HALVES], F32, name="gate_cols")
+            nc.vector.tensor_copy(gate_cols[:], gate_bank[:, : D * HALVES])
+            gates = []
+            for g in range(D // 2):
+                gate_bank = psum.tile([P, T], F32, name="bank")
+                for e in range(2):
+                    for v in range(HALVES):
+                        j = D * v + 2 * g + e
+                        nc.tensor.transpose(
+                            gate_bank[:, (2 * e + v) * P : (2 * e + v + 1) * P],
+                            gate_cols[:, j : j + 1].to_broadcast([P, P]),
+                            ident[:],
+                        )
+                pair = keep.tile([P, 2, V], F32, name=f"gates{g}")
+                nc.scalar.copy(pair[:].rearrange("p e v -> p (e v)"), gate_bank[:])
+                gates.append(pair)
+            return gates
 
         xq = []
         for c in range(PASSES):
             grouped = keep.tile([P, T, 4], BF16, name=f"xg{c}", align_bytes=64)
             codes = keep.tile([P, T], U32, name=f"xq{c}", align_bytes=64)
             scales = keep.tile([P, T], U8, name=f"xs{c}", align_bytes=64)
-            cut = 256
+            cut = 160
             nc.scalar.copy(
                 grouped[:, :cut, :].rearrange("p (c i) t -> p c t i", i=4),
                 xraw[c][:, :, :cut].rearrange("p t (c i) -> p c t i", i=4),
@@ -92,99 +111,120 @@ def tile_picked_gcn_mlp_none_sub_l_kernel(tc, xT, w1, w2, gate, pos1, pos2, pos3
             )
             nc.vector.quantize_mx(out=codes[:].bitcast(FP8X4), scales=scales[:], in_=grouped[:].rearrange("p w t -> p (w t)"))
             xq.append((codes, scales))
+            if c == 1:
+                gates = spread_gates()
 
         wg = [[keep.tile([P, 2, P, 4], BF16, name=f"wg{b}_{s}", align_bytes=64) for s in range(2)] for b in range(BLOCKS)]
         wq = [[keep.tile([P, 2, P], U32, name=f"wq{b}_{s}", align_bytes=64) for s in range(2)] for b in range(BLOCKS)]
         ws = [[keep.tile([P, 2, P], U8, name=f"ws{b}_{s}", align_bytes=64) for s in range(2)] for b in range(BLOCKS)]
         h = [keep.tile([P, T], F32, name=f"h{b}") for b in range(BLOCKS)]
-        hps = {}
 
-        def multiply(b, c):
-            if c == 0:
-                hps[b] = psum.tile([P, T], F32, name="bank")
+        def multiply(bank, b, c, nodes):
             nc.tensor.matmul_mx(
-                out=hps[b][:],
+                out=bank,
                 lhsT=wq[b][c // 2][:, c % 2, :].bitcast(FP8X4),
                 lhsT_scale=ws[b][c // 2][:, c % 2, :],
-                rhs=xq[c][0][:].bitcast(FP8X4),
-                rhs_scale=xq[c][1][:],
+                rhs=xq[c][0][:, nodes].bitcast(FP8X4),
+                rhs_scale=xq[c][1][:, nodes],
                 start=(c == 0),
                 stop=(c == PASSES - 1),
             )
 
+        node_halves = (slice(0, T // 2), slice(T // 2, T))
+        first = [psum.tile([P, T], F32, name="bank") for n in range(2)]
+        def interleave(copy, b, c, columns):
+            copy(
+                wg[b][c // 2][:, c % 2, columns, :].rearrange("p (c i) t -> p c t i", i=4),
+                wraw[b][c // 2][:, c % 2, :, columns].rearrange("p t (c i) -> p c t i", i=4),
+            )
+
+        def quantise_w1(b, s, part):
+            nc.vector.quantize_mx(
+                out=wq[b][s][:, part, :].rearrange("p c w -> p (c w)").bitcast(FP8X4),
+                scales=ws[b][s][:, part, :].rearrange("p c w -> p (c w)"),
+                in_=wg[b][s][:, part, :, :].rearrange("p c w t -> p (c w t)"),
+            )
+
+        for c in range(PASSES - 1):
+            interleave(nc.scalar.copy, 0, c, slice(0, P))
+        interleave(nc.scalar.copy, 0, PASSES - 1, slice(0, 48))
+        interleave(nc.vector.tensor_copy, 0, PASSES - 1, slice(48, P))
+        quantise_w1(0, 0, slice(0, 2))
+        quantise_w1(0, 1, slice(0, 1))
+        quantise_w1(0, 1, slice(1, 2))
         for c in range(PASSES):
-            src = wraw[0][c // 2][:, c % 2, :, :]
-            dst = wg[0][c // 2][:, c % 2, :, :]
-            nc.scalar.copy(dst[:, :64, :].rearrange("p (c i) t -> p c t i", i=4), src[:, :, :64].rearrange("p t (c i) -> p c t i", i=4))
-            nc.vector.tensor_copy(dst[:, 64:, :].rearrange("p (c i) t -> p c t i", i=4), src[:, :, 64:].rearrange("p t (c i) -> p c t i", i=4))
-            nc.vector.quantize_mx(
-                out=wq[0][c // 2][:, c % 2, :].bitcast(FP8X4),
-                scales=ws[0][c // 2][:, c % 2, :],
-                in_=dst.rearrange("p w t -> p (w t)"),
-            )
-            multiply(0, c)
-        nc.scalar.copy(h[0][:], hps[0][:])
-
-        def copy_w1(b, s):
-            nc.scalar.copy(wg[b][s][:], wraw[b][s][:].rearrange("p c t w -> p c w t"))
-
-        def quantise_w1(b, s):
-            nc.vector.quantize_mx(
-                out=wq[b][s][:].rearrange("p c w -> p (c w)").bitcast(FP8X4),
-                scales=ws[b][s][:].rearrange("p c w -> p (c w)"),
-                in_=wg[b][s][:].rearrange("p c w t -> p (c w t)"),
-            )
-            multiply(b, 2 * s)
-            multiply(b, 2 * s + 1)
+            for n in range(2):
+                multiply(first[n][:, : T // 2], 0, c, node_halves[n])
+        for n in range(2):
+            nc.vector.tensor_copy(h[0][:, node_halves[n]], first[n][:, : T // 2])
 
         w2g = keep.tile([P, N, 4], BF16, name="w2g", align_bytes=64)
         w2q = keep.tile([P, N], U32, name="w2q", align_bytes=64)
         w2s = keep.tile([P, N], U8, name="w2s", align_bytes=64)
-        zT = [keep.tile([P, 4, P], BF16, name=f"zT{v}") for v in range(HALVES)]
+        zT = [keep.tile([P, 2, P, 2], BF16, name=f"zT{v}") for v in range(HALVES)]
 
-        for b in range(BLOCKS):
-            if b + 1 < BLOCKS:
-                copy_w1(b + 1, 0)
-                copy_w1(b + 1, 1)
-            else:
-                nc.scalar.copy(w2g[:], w2raw[:].rearrange("p t m -> p m t"))
+        def gather(b, d, targets, picked):
+            nc.vector.tensor_tensor(
+                picked, h[b][:].indirect(pos[d][:, targets.start // 16 : targets.stop // 16]), gates[d // 2][:, d % 2, targets], MULT
+            )
+
+        def add_turned(acc, picked, d):
+            nc.tensor.matmul(acc, picked, ident[:], is_transpose=True, start=(d == 0), stop=(d == D - 1))
+
+        def round_sums(copy, b, v, acc):
+            copy(zT[v][:, :, 32 * b : 32 * (b + 1), :], acc.rearrange("r (q u e) -> r u q e", u=2, e=2))
+
+        for b in range(BLOCKS - 1):
+            for c in range(PASSES):
+                interleave(nc.scalar.copy, b + 1, c, slice(0, P))
+            bank = psum.tile([P, T], F32, name="bank")
             acc = [psum.tile([P, P], F32, name=f"acc{v}") for v in range(HALVES)]
             for d in range(D):
                 picked = ring.tile([P, V], F32, name="picked")
-                nc.vector.tensor_tensor(picked[:], h[b][:].indirect(pos[d][:]), gates[d // 2][:, d % 2, :], MULT)
+                gather(b, d, slice(0, V), picked[:])
                 for v in range(HALVES):
-                    nc.tensor.matmul(
-                        acc[v][:], picked[:, P * v : P * (v + 1)], ident_f32[:],
-                        is_transpose=True, start=(d == 0), stop=(d == D - 1),
-                    )
-                if b + 1 < BLOCKS:
-                    if d == 1:
-                        quantise_w1(b + 1, 0)
-                    if d == 4:
-                        quantise_w1(b + 1, 1)
-                        nc.scalar.copy(h[b + 1][:], hps[b + 1][:])
-                elif d == 2:
-                    nc.vector.quantize_mx(out=w2q[:].bitcast(FP8X4), scales=w2s[:], in_=w2g[:].rearrange("p m t -> p (m t)"))
+                    add_turned(acc[v][:], picked[:, P * v : P * (v + 1)], d)
+                if d == 1:
+                    quantise_w1(b + 1, 0, slice(0, 2))
+                    multiply(bank[:], b + 1, 0, slice(0, T))
+                    multiply(bank[:], b + 1, 1, slice(0, T))
+                if d == 3:
+                    quantise_w1(b + 1, 1, slice(0, 2))
+                    multiply(bank[:], b + 1, 2, slice(0, T))
+                    multiply(bank[:], b + 1, 3, slice(0, T))
+                    nc.scalar.copy(h[b + 1][:], bank[:])
             for v in range(HALVES):
-                dst = zT[v][:, :, 32 * b : 32 * (b + 1)]
-                src = acc[v][:].rearrange("p (q t) -> p t q", t=4)
-                if v == 1 and b == BLOCKS - 1:
-                    nc.vector.tensor_copy(dst, src)
-                else:
-                    nc.scalar.copy(dst, src)
+                round_sums(nc.scalar.copy, b, v, acc[v][:])
+            if b == 1:
+                nc.scalar.copy(w2g[:], w2raw[:].rearrange("p t m -> p m t"))
+            if b == 2:
+                nc.vector.quantize_mx(out=w2q[:].bitcast(FP8X4), scales=w2s[:], in_=w2g[:].rearrange("p m t -> p (m t)"))
 
-        zbank = [psum1.tile([P, 4, P], BF16, name=f"zbank{v}") for v in range(HALVES)]
+        b = BLOCKS - 1
+        zbank = [psum1.tile([P, 2, P], F32, name=f"zbank{v}") for v in range(HALVES)]
         zg = [keep.tile([P, P, 4], BF16, name=f"zg{v}", align_bytes=64) for v in range(HALVES)]
         zq = [keep.tile([P, P], U32, name=f"zq{v}", align_bytes=64) for v in range(HALVES)]
         zs = [keep.tile([P, P], U8, name=f"zs{v}", align_bytes=64) for v in range(HALVES)]
         result = [keep.tile([P, P], F32, name=f"result{v}") for v in range(HALVES)]
-        for v in range(HALVES):
-            for t in range(4):
-                nc.tensor.transpose(zbank[v][:, t, :], zT[v][:, t, :], ident_bf16[:])
-        nc.scalar.copy(zg[0][:], zbank[0][:].rearrange("p t v -> p v t"))
-        nc.vector.tensor_copy(zg[1][:], zbank[1][:].rearrange("p t v -> p v t"))
-        for v in range(HALVES):
-            nc.vector.quantize_mx(out=zq[v][:].bitcast(FP8X4), scales=zs[v][:], in_=zg[v][:].rearrange("p v t -> p (v t)"))
+        acc = [psum.tile([P, P], F32, name=f"acc{v}") for v in range(HALVES)]
+
+        def pick_half(v):
+            for d in range(D):
+                picked = ring.tile([P, P], F32, name="picked_half")
+                gather(b, d, slice(P * v, P * (v + 1)), picked[:])
+                add_turned(acc[v][:], picked[:], d)
+
+        def turn_back(v):
+            words = zT[v][:].rearrange("r u p e -> r (u p e)").bitcast(F32)
+            for u in range(2):
+                nc.tensor.transpose(zbank[v][:, u, :], words[:, P * u : P * (u + 1)], ident[:])
+            nc.scalar.copy(
+                zg[v][:].rearrange("p r t -> p (r t)").bitcast(F32).rearrange("p (r u) -> p r u", u=2),
+                zbank[v][:].rearrange("p u r -> p r u"),
+            )
+
+        def second_layer(v, copy, queue):
+            nc.vector.quantize_mx(out=zq[v][:].bitcast(FP8X4), scales=zs[v][:], in_=zg[v][:].rearrange("p r t -> p (r t)"))
             bank = psum.tile([P, T], F32, name="bank")
             nc.tensor.matmul_mx(
                 out=bank[:, :P],
@@ -192,9 +232,14 @@ def tile_picked_gcn_mlp_none_sub_l_kernel(tc, xT, w1, w2, gate, pos1, pos2, pos3
                 rhs=zq[v][:].bitcast(FP8X4), rhs_scale=zs[v][:],
                 start=True, stop=True,
             )
-            if v == 0:
-                nc.scalar.copy(result[v][:], bank[:, :P])
-                nc.scalar.dma_start(out=out[:, :P], in_=result[v][:])
-            else:
-                nc.vector.tensor_copy(result[v][:], bank[:, :P])
-                nc.sync.dma_start(out=out[:, P:], in_=result[v][:])
+            copy(result[v][:], bank[:, :P])
+            queue.dma_start(out=out[:, P * v : P * (v + 1)], in_=result[v][:])
+
+        pick_half(0)
+        round_sums(nc.scalar.copy, b, 0, acc[0][:])
+        turn_back(0)
+        pick_half(1)
+        second_layer(0, nc.scalar.copy, nc.sync)
+        round_sums(nc.vector.tensor_copy, b, 1, acc[1][:])
+        turn_back(1)
+        second_layer(1, nc.vector.tensor_copy, nc.sync)

@@ -27,7 +27,7 @@ def tile_picked_gcn_mlp_none_sub_l_kernel(tc, xT, w1, w2, gate, pos1, pos2, pos3
     with ExitStack() as ctx:
         lists = ctx.enter_context(tc.tile_pool(name="lists", bufs=1))
         keep = ctx.enter_context(tc.tile_pool(name="keep", bufs=1))
-        ring = ctx.enter_context(tc.tile_pool(name="ring", bufs=4))
+        turns = ctx.enter_context(tc.tile_pool(name="turns", bufs=1))
         psum = ctx.enter_context(tc.psum_pool(name="psum", bufs=2))
         psum1 = ctx.enter_context(tc.psum_pool(name="psum1", bufs=1))
 
@@ -114,7 +114,6 @@ def tile_picked_gcn_mlp_none_sub_l_kernel(tc, xT, w1, w2, gate, pos1, pos2, pos3
             if c == 1:
                 gates = spread_gates()
 
-        wg = [[keep.tile([P, 2, P, 4], BF16, name=f"wg{b}_{s}", align_bytes=64) for s in range(2)] for b in range(BLOCKS)]
         wq = [[keep.tile([P, 2, P], U32, name=f"wq{b}_{s}", align_bytes=64) for s in range(2)] for b in range(BLOCKS)]
         ws = [[keep.tile([P, 2, P], U8, name=f"ws{b}_{s}", align_bytes=64) for s in range(2)] for b in range(BLOCKS)]
         h = [keep.tile([P, T], F32, name=f"h{b}") for b in range(BLOCKS)]
@@ -130,33 +129,28 @@ def tile_picked_gcn_mlp_none_sub_l_kernel(tc, xT, w1, w2, gate, pos1, pos2, pos3
                 stop=(c == PASSES - 1),
             )
 
-        node_halves = (slice(0, T // 2), slice(T // 2, T))
-        first = [psum.tile([P, T], F32, name="bank") for n in range(2)]
-        def interleave(copy, b, c, columns):
+        bank = psum.tile([P, T], F32, name="bank")
+        def interleave(copy, grouped, b, c, columns):
             copy(
-                wg[b][c // 2][:, c % 2, columns, :].rearrange("p (c i) t -> p c t i", i=4),
+                grouped[:, columns, :].rearrange("p (c i) t -> p c t i", i=4),
                 wraw[b][c // 2][:, c % 2, :, columns].rearrange("p t (c i) -> p c t i", i=4),
             )
 
-        def quantise_w1(b, s, part):
+        def quantise_w1(grouped, b, passes):
+            part = slice(passes[0] % 2, passes[-1] % 2 + 1)
             nc.vector.quantize_mx(
-                out=wq[b][s][:, part, :].rearrange("p c w -> p (c w)").bitcast(FP8X4),
-                scales=ws[b][s][:, part, :].rearrange("p c w -> p (c w)"),
-                in_=wg[b][s][:, part, :, :].rearrange("p c w t -> p (c w t)"),
+                out=wq[b][passes[0] // 2][:, part, :].rearrange("p c w -> p (c w)").bitcast(FP8X4),
+                scales=ws[b][passes[0] // 2][:, part, :].rearrange("p c w -> p (c w)"),
+                in_=grouped.rearrange("p c w t -> p (c w t)"),
             )
 
-        for c in range(PASSES - 1):
-            interleave(nc.scalar.copy, 0, c, slice(0, P))
-        interleave(nc.scalar.copy, 0, PASSES - 1, slice(0, 48))
-        interleave(nc.vector.tensor_copy, 0, PASSES - 1, slice(48, P))
-        quantise_w1(0, 0, slice(0, 2))
-        quantise_w1(0, 1, slice(0, 1))
-        quantise_w1(0, 1, slice(1, 2))
         for c in range(PASSES):
-            for n in range(2):
-                multiply(first[n][:, : T // 2], 0, c, node_halves[n])
-        for n in range(2):
-            nc.vector.tensor_copy(h[0][:, node_halves[n]], first[n][:, : T // 2])
+            grouped = keep.tile([P, 1, P, 4], BF16, name=f"wg{c}", align_bytes=64)
+            interleave(nc.scalar.copy, grouped[:, 0], 0, c, slice(0, 64))
+            interleave(nc.vector.tensor_copy, grouped[:, 0], 0, c, slice(64, P))
+            quantise_w1(grouped[:], 0, (c,))
+            multiply(bank[:], 0, c, slice(0, T))
+        nc.vector.tensor_copy(h[0][:], bank[:])
 
         w2g = keep.tile([P, N, 4], BF16, name="w2g", align_bytes=64)
         w2q = keep.tile([P, N], U32, name="w2q", align_bytes=64)
@@ -174,25 +168,30 @@ def tile_picked_gcn_mlp_none_sub_l_kernel(tc, xT, w1, w2, gate, pos1, pos2, pos3
         def round_sums(copy, b, v, acc):
             copy(zT[v][:, :, 32 * b : 32 * (b + 1), :], acc.rearrange("r (q u e) -> r u q e", u=2, e=2))
 
+        parts = {1: (((0, 1), 1), ((2,), 2), ((3,), 3)), 2: (((0, 1), 1), ((2, 3), 2)), 3: (((0, 1), 1), ((2, 3), 2))}
         for b in range(BLOCKS - 1):
-            for c in range(PASSES):
-                interleave(nc.scalar.copy, b + 1, c, slice(0, P))
+            waiting = {}
+            for k, (passes, d) in enumerate(parts[b + 1]):
+                grouped = turns.tile([P, len(passes), P, 4], BF16, name=f"turn{k}", align_bytes=64)
+                for e, c in enumerate(passes):
+                    interleave(nc.scalar.copy, grouped[:, e], b + 1, c, slice(0, P))
+                waiting[d] = (k, passes, grouped)
             bank = psum.tile([P, T], F32, name="bank")
             acc = [psum.tile([P, P], F32, name=f"acc{v}") for v in range(HALVES)]
             for d in range(D):
-                picked = ring.tile([P, V], F32, name="picked")
+                if d in waiting:
+                    k, passes, grouped = waiting[d]
+                    quantise_w1(grouped[:], b + 1, passes)
+                    for c in passes:
+                        multiply(bank[:], b + 1, c, slice(0, T))
+                    if passes[-1] == PASSES - 1:
+                        nc.scalar.copy(h[b + 1][:], bank[:])
+                    picked = turns.tile([P, V], F32, name=f"turn{k}", align_bytes=64)
+                else:
+                    picked = keep.tile([P, V], F32, name=f"picked{b}_{d}")
                 gather(b, d, slice(0, V), picked[:])
                 for v in range(HALVES):
                     add_turned(acc[v][:], picked[:, P * v : P * (v + 1)], d)
-                if d == 1:
-                    quantise_w1(b + 1, 0, slice(0, 2))
-                    multiply(bank[:], b + 1, 0, slice(0, T))
-                    multiply(bank[:], b + 1, 1, slice(0, T))
-                if d == 3:
-                    quantise_w1(b + 1, 1, slice(0, 2))
-                    multiply(bank[:], b + 1, 2, slice(0, T))
-                    multiply(bank[:], b + 1, 3, slice(0, T))
-                    nc.scalar.copy(h[b + 1][:], bank[:])
             for v in range(HALVES):
                 round_sums(nc.scalar.copy, b, v, acc[v][:])
             if b == 1:
@@ -210,7 +209,7 @@ def tile_picked_gcn_mlp_none_sub_l_kernel(tc, xT, w1, w2, gate, pos1, pos2, pos3
 
         def pick_half(v):
             for d in range(D):
-                picked = ring.tile([P, P], F32, name="picked_half")
+                picked = keep.tile([P, P], F32, name=f"picked{b}_{d}_{v}")
                 gather(b, d, slice(P * v, P * (v + 1)), picked[:])
                 add_turned(acc[v][:], picked[:], d)
 

@@ -114,15 +114,14 @@ def tile_picked_gcn_mlp_none_sub_l_kernel(tc, xT, w1, w2, gate, pos1, pos2, pos3
             if c == 1:
                 gates = spread_gates()
 
-        wq = [[keep.tile([P, 2, P], U32, name=f"wq{b}_{s}", align_bytes=64) for s in range(2)] for b in range(BLOCKS)]
-        ws = [[keep.tile([P, 2, P], U8, name=f"ws{b}_{s}", align_bytes=64) for s in range(2)] for b in range(BLOCKS)]
+        wq = {}
         h = [keep.tile([P, T], F32, name=f"h{b}") for b in range(BLOCKS)]
 
         def multiply(bank, b, c, nodes):
             nc.tensor.matmul_mx(
                 out=bank,
-                lhsT=wq[b][c // 2][:, c % 2, :].bitcast(FP8X4),
-                lhsT_scale=ws[b][c // 2][:, c % 2, :],
+                lhsT=wq[b, c][0].bitcast(FP8X4),
+                lhsT_scale=wq[b, c][1],
                 rhs=xq[c][0][:, nodes].bitcast(FP8X4),
                 rhs_scale=xq[c][1][:, nodes],
                 start=(c == 0),
@@ -137,12 +136,16 @@ def tile_picked_gcn_mlp_none_sub_l_kernel(tc, xT, w1, w2, gate, pos1, pos2, pos3
             )
 
         def quantise_w1(grouped, b, passes):
-            part = slice(passes[0] % 2, passes[-1] % 2 + 1)
+            n = len(passes)
+            codes = keep.tile([P, n, P], U32, name=f"wq{b}_{passes[0]}", align_bytes=64)
+            scales = keep.tile([P, n, P], U8, name=f"ws{b}_{passes[0]}", align_bytes=64)
             nc.vector.quantize_mx(
-                out=wq[b][passes[0] // 2][:, part, :].rearrange("p c w -> p (c w)").bitcast(FP8X4),
-                scales=ws[b][passes[0] // 2][:, part, :].rearrange("p c w -> p (c w)"),
+                out=codes[:].rearrange("p c w -> p (c w)").bitcast(FP8X4),
+                scales=scales[:].rearrange("p c w -> p (c w)"),
                 in_=grouped.rearrange("p c w t -> p (c w t)"),
             )
+            for e, c in enumerate(passes):
+                wq[b, c] = (codes[:, e, :], scales[:, e, :])
 
         for c in range(PASSES):
             grouped = keep.tile([P, 1, P, 4], BF16, name=f"wg{c}", align_bytes=64)
@@ -168,11 +171,11 @@ def tile_picked_gcn_mlp_none_sub_l_kernel(tc, xT, w1, w2, gate, pos1, pos2, pos3
         def round_sums(copy, b, v, acc):
             copy(zT[v][:, :, 32 * b : 32 * (b + 1), :], acc.rearrange("r (q u e) -> r u q e", u=2, e=2))
 
-        parts = {1: (((0, 1), 1), ((2,), 2), ((3,), 3)), 2: (((0, 1), 1), ((2, 3), 2)), 3: (((0, 1), 1), ((2, 3), 2))}
+        parts = {b: (((0, 1), 0), ((2, 3), 1)) for b in (1, 2, 3)}
         for b in range(BLOCKS - 1):
             waiting = {}
             for k, (passes, d) in enumerate(parts[b + 1]):
-                grouped = turns.tile([P, len(passes), P, 4], BF16, name=f"turn{k}", align_bytes=64)
+                grouped = turns.tile([P, len(passes), P, 4], BF16, name=f"turn{b}_{k}", align_bytes=64)
                 for e, c in enumerate(passes):
                     interleave(nc.scalar.copy, grouped[:, e], b + 1, c, slice(0, P))
                 waiting[d] = (k, passes, grouped)
@@ -186,7 +189,7 @@ def tile_picked_gcn_mlp_none_sub_l_kernel(tc, xT, w1, w2, gate, pos1, pos2, pos3
                         multiply(bank[:], b + 1, c, slice(0, T))
                     if passes[-1] == PASSES - 1:
                         nc.scalar.copy(h[b + 1][:], bank[:])
-                    picked = turns.tile([P, V], F32, name=f"turn{k}", align_bytes=64)
+                    picked = turns.tile([P, V], F32, name=f"turn{b}_{k}", align_bytes=64)
                 else:
                     picked = keep.tile([P, V], F32, name=f"picked{b}_{d}")
                 gather(b, d, slice(0, V), picked[:])

from contextlib import ExitStack

import concourse.mybir as mybir
from concourse.masks import make_identity

K, T, D, V, H, N = 2048, 512, 6, 256, 512, 128
P = 128
PASSES = K // 512
BLOCKS = H // P
HALVES = V // P
FLOPS = 2 * K * H * T + 2 * H * N * V
BYTES = 4 * (K * T + K * H + H * N + D * V + N * V) + 2 * D * P * (V // 16)

F32 = mybir.dt.float32
BF16 = mybir.dt.bfloat16
U32 = mybir.dt.uint32
U16 = mybir.dt.uint16
U8 = mybir.dt.uint8
FP8X4 = mybir.dt.float8_e4m3fn_x4
MULT = mybir.AluOpType.mult


def tile_picked_gcn_mlp_none_sub_l_kernel(tc, xT, w1, w2, gate, pos1, pos2, pos3, pos4, pos5, pos6, out):
    nc = tc.nc
    lists_in = (pos1, pos2, pos3, pos4, pos5, pos6)

    with ExitStack() as ctx:
        lists = ctx.enter_context(tc.tile_pool(name="lists", bufs=1))
        keep = ctx.enter_context(tc.tile_pool(name="keep", bufs=1))
        turns = ctx.enter_context(tc.tile_pool(name="turns", bufs=1))
        psum = ctx.enter_context(tc.psum_pool(name="psum", bufs=2))
        psum1 = ctx.enter_context(tc.psum_pool(name="psum1", bufs=1))

        pos = [lists.tile([P, V // 16], U16, name=f"pos{d}") for d in range(D)]

        xraw = [keep.tile([P, 4, T], F32, name=f"xraw{c}") for c in range(PASSES)]
        wraw = [[keep.tile([P, 2, 4, P], F32, name=f"wraw{b}_{s}") for s in range(2)] for b in range(BLOCKS)]
        w2raw = keep.tile([P, 4, N], F32, name="w2raw")
        gate_rows = keep.tile([P, P], F32, name="gate_rows")
        nc.gpsimd.memset(gate_rows[:], 0.0)

        def load_w1(b, c):
            nc.sync.dma_start(
                out=wraw[b][c // 2][:, c % 2, :, :],
                in_=w1[512 * c : 512 * (c + 1), P * b : P * (b + 1)].rearrange("(p j) w -> p j w", j=4),
            )

        def load_list(d):
            nc.sync.dma_start(pos[d][:], lists_in[d])

        for c in range(PASSES):
            nc.sync.dma_start(out=xraw[c][:], in_=xT[512 * c : 512 * (c + 1), :].rearrange("(p j) w -> p j w", j=4))
            if c == 0:
                for v in range(HALVES):
                    nc.sync.dma_start(out=gate_rows[D * v : D * (v + 1), :], in_=gate[:, 0, P * v : P * (v + 1)])
        for c in range(PASSES):
            load_w1(0, c)
        load_list(0)
        load_list(1)
        load_w1(1, 0)
        load_list(2)
        load_w1(1, 1)
        load_list(3)
        load_w1(1, 2)
        load_list(4)
        load_list(5)
        load_w1(1, 3)
        for c in range(PASSES):
            load_w1(2, c)
        nc.sync.dma_start(out=w2raw[:], in_=w2.rearrange("(p j) m -> p j m", j=4))
        for c in range(PASSES):
            load_w1(3, c)

        ident = keep.tile([P, P], F32, name="ident")
        make_identity(nc, ident[:])

        def spread_gates():
            gate_bank = psum.tile([P, T], F32, name="bank")
            nc.tensor.transpose(gate_bank[:, :P], gate_rows[:], ident[:])
            gate_cols = keep.tile([P, D * HALVES], F32, name="gate_cols")
            nc.vector.tensor_copy(gate_cols[:], gate_bank[:, : D * HALVES])
            gates = []
            for g in range(D // 2):
                gate_bank = psum.tile([P, T], F32, name="bank")
                for e in range(2):
                    for v in range(HALVES):
                        j = D * v + 2 * g + e
                        nc.tensor.transpose(
                            gate_bank[:, (2 * e + v) * P : (2 * e + v + 1) * P],
                            gate_cols[:, j : j + 1].to_broadcast([P, P]),
                            ident[:],
                        )
                pair = keep.tile([P, 2, V], F32, name=f"gates{g}")
                nc.scalar.copy(pair[:].rearrange("p e v -> p (e v)"), gate_bank[:])
                gates.append(pair)
            return gates

        xq = []
        for c in range(PASSES):
            grouped = keep.tile([P, T, 4], BF16, name=f"xg{c}", align_bytes=64)
            codes = keep.tile([P, T], U32, name=f"xq{c}", align_bytes=64)
            scales = keep.tile([P, T], U8, name=f"xs{c}", align_bytes=64)
            cut = 160
            nc.scalar.copy(
                grouped[:, :cut, :].rearrange("p (c i) t -> p c t i", i=4),
                xraw[c][:, :, :cut].rearrange("p t (c i) -> p c t i", i=4),
            )
            nc.vector.tensor_copy(
                grouped[:, cut:, :].rearrange("p (c i) t -> p c t i", i=4),
                xraw[c][:, :, cut:].rearrange("p t (c i) -> p c t i", i=4),
            )
            nc.vector.quantize_mx(out=codes[:].bitcast(FP8X4), scales=scales[:], in_=grouped[:].rearrange("p w t -> p (w t)"))
            xq.append((codes, scales))
            if c == 1:
                gates = spread_gates()

        wq = {}
        h = [keep.tile([P, T], F32, name=f"h{b}") for b in range(BLOCKS)]

        def multiply(bank, b, c, nodes):
            nc.tensor.matmul_mx(
                out=bank,
                lhsT=wq[b, c][0].bitcast(FP8X4),
                lhsT_scale=wq[b, c][1],
                rhs=xq[c][0][:, nodes].bitcast(FP8X4),
                rhs_scale=xq[c][1][:, nodes],
                start=(c == 0),
                stop=(c == PASSES - 1),
            )

        bank = psum.tile([P, T], F32, name="bank")
        def interleave(copy, grouped, b, c, columns):
            copy(
                grouped[:, columns, :].rearrange("p (c i) t -> p c t i", i=4),
                wraw[b][c // 2][:, c % 2, :, columns].rearrange("p t (c i) -> p c t i", i=4),
            )

        def quantise_w1(grouped, b, passes):
            n = len(passes)
            codes = keep.tile([P, n, P], U32, name=f"wq{b}_{passes[0]}", align_bytes=64)
            scales = keep.tile([P, n, P], U8, name=f"ws{b}_{passes[0]}", align_bytes=64)
            nc.vector.quantize_mx(
                out=codes[:].rearrange("p c w -> p (c w)").bitcast(FP8X4),
                scales=scales[:].rearrange("p c w -> p (c w)"),
                in_=grouped.rearrange("p c w t -> p (c w t)"),
            )
            for e, c in enumerate(passes):
                wq[b, c] = (codes[:, e, :], scales[:, e, :])

        for c in range(PASSES):
            grouped = keep.tile([P, 1, P, 4], BF16, name=f"wg{c}", align_bytes=64)
            interleave(nc.scalar.copy, grouped[:, 0], 0, c, slice(0, 64))
            interleave(nc.vector.tensor_copy, grouped[:, 0], 0, c, slice(64, P))
            quantise_w1(grouped[:], 0, (c,))
            multiply(bank[:], 0, c, slice(0, T))
        nc.vector.tensor_copy(h[0][:], bank[:])

        w2g = keep.tile([P, N, 4], BF16, name="w2g", align_bytes=64)
        w2q = keep.tile([P, N], U32, name="w2q", align_bytes=64)
        w2s = keep.tile([P, N], U8, name="w2s", align_bytes=64)
        zT = [keep.tile([P, 2, P, 2], BF16, name=f"zT{v}") for v in range(HALVES)]

        def gather(b, d, targets, picked):
            nc.vector.tensor_tensor(
                picked, h[b][:].indirect(pos[d][:, targets.start // 16 : targets.stop // 16]), gates[d // 2][:, d % 2, targets], MULT
            )

        def add_turned(acc, picked, d):
            nc.tensor.matmul(acc, picked, ident[:], is_transpose=True, start=(d == 0), stop=(d == D - 1))

        def round_sums(copy, b, v, acc):
            copy(zT[v][:, :, 32 * b : 32 * (b + 1), :], acc.rearrange("r (q u e) -> r u q e", u=2, e=2))

        parts = {b: (((0, 1), 0), ((2, 3), 1)) for b in (1, 2, 3)}
        for b in range(BLOCKS - 1):
            waiting = {}
            for k, (passes, d) in enumerate(parts[b + 1]):
                grouped = turns.tile([P, len(passes), P, 4], BF16, name=f"turn{b}_{k}", align_bytes=64)
                for e, c in enumerate(passes):
                    interleave(nc.scalar.copy, grouped[:, e], b + 1, c, slice(0, P))
                waiting[d] = (k, passes, grouped)
            bank = psum.tile([P, T], F32, name="bank")
            acc = [psum.tile([P, P], F32, name=f"acc{v}") for v in range(HALVES)]
            for d in range(D):
                if d in waiting:
                    k, passes, grouped = waiting[d]
                    quantise_w1(grouped[:], b + 1, passes)
                    for c in passes:
                        multiply(bank[:], b + 1, c, slice(0, T))
                    if passes[-1] == PASSES - 1:
                        nc.scalar.copy(h[b + 1][:], bank[:])
                    picked = turns.tile([P, V], F32, name=f"turn{b}_{k}", align_bytes=64)
                else:
                    picked = keep.tile([P, V], F32, name=f"picked{b}_{d}")
                gather(b, d, slice(0, V), picked[:])
                for v in range(HALVES):
                    add_turned(acc[v][:], picked[:, P * v : P * (v + 1)], d)
            for v in range(HALVES):
                round_sums(nc.scalar.copy, b, v, acc[v][:])
            if b == 1:
                nc.scalar.copy(w2g[:], w2raw[:].rearrange("p t m -> p m t"))
            if b == 2:
                nc.vector.quantize_mx(out=w2q[:].bitcast(FP8X4), scales=w2s[:], in_=w2g[:].rearrange("p m t -> p (m t)"))

        b = BLOCKS - 1
        zbank = [psum1.tile([P, 2, P], F32, name=f"zbank{v}") for v in range(HALVES)]
        zg = [keep.tile([P, P, 4], BF16, name=f"zg{v}", align_bytes=64) for v in range(HALVES)]
        zq = [keep.tile([P, P], U32, name=f"zq{v}", align_bytes=64) for v in range(HALVES)]
        zs = [keep.tile([P, P], U8, name=f"zs{v}", align_bytes=64) for v in range(HALVES)]
        result = [keep.tile([P, P], F32, name=f"result{v}") for v in range(HALVES)]
        acc = [psum.tile([P, P], F32, name=f"acc{v}") for v in range(HALVES)]

        def pick_half(v):
            for d in range(D):
                picked = keep.tile([P, P], F32, name=f"picked{b}_{d}_{v}")
                gather(b, d, slice(P * v, P * (v + 1)), picked[:])
                add_turned(acc[v][:], picked[:], d)

        def turn_back(v):
            words = zT[v][:].rearrange("r u p e -> r (u p e)").bitcast(F32)
            for u in range(2):
                nc.tensor.transpose(zbank[v][:, u, :], words[:, P * u : P * (u + 1)], ident[:])
            nc.scalar.copy(
                zg[v][:].rearrange("p r t -> p (r t)").bitcast(F32).rearrange("p (r u) -> p r u", u=2),
                zbank[v][:].rearrange("p u r -> p r u"),
            )

        def second_layer(v, copy, queue):
            nc.vector.quantize_mx(out=zq[v][:].bitcast(FP8X4), scales=zs[v][:], in_=zg[v][:].rearrange("p r t -> p (r t)"))
            bank = psum.tile([P, T], F32, name="bank")
            nc.tensor.matmul_mx(
                out=bank[:, :P],
                lhsT=w2q[:].bitcast(FP8X4), lhsT_scale=w2s[:],
                rhs=zq[v][:].bitcast(FP8X4), rhs_scale=zs[v][:],
                start=True, stop=True,
            )
            copy(result[v][:], bank[:, :P])
            queue.dma_start(out=out[:, P * v : P * (v + 1)], in_=result[v][:])

        pick_half(0)
        round_sums(nc.scalar.copy, b, 0, acc[0][:])
        turn_back(0)
        pick_half(1)
        second_layer(0, nc.scalar.copy, nc.sync)
        round_sums(nc.vector.tensor_copy, b, 1, acc[1][:])
        turn_back(1)
        second_layer(1, nc.vector.tensor_copy, nc.sync)
